import numpy as np
import ml_dtypes


def mxq(x, axis, fmt="e4m3"):
    dtype, down = {"e4m3": (ml_dtypes.float8_e4m3fn, 7), "e5m2": (ml_dtypes.float8_e5m2, 14)}[fmt]
    v = np.moveaxis(np.asarray(x, np.float32).astype(ml_dtypes.bfloat16).astype(np.float64), axis, -1)
    blocks = v.reshape(v.shape[:-1] + (-1, 32))
    amax = np.abs(blocks).max(-1, keepdims=True)
    byte = np.maximum(np.where(amax > 0, np.frexp(amax)[1] - 1 + 127, 0) - down, 1)
    scale = np.exp2(byte - 127.0)
    codes = (blocks / scale).astype(np.float32).astype(dtype).astype(np.float64)
    return np.moveaxis((codes * scale).reshape(v.shape), -1, axis)


WIDE = False


def mx_kscale(k):
    if not WIDE:
        return np.ones(k)
    levels = np.array([10, -10, 5, -5, 0])
    if k % 512:
        return np.exp2(np.random.permutation(np.resize(levels, k // 32))).repeat(32)
    a = np.empty((k // 512, 16))
    for p in range(k // 512):
        a[p, :8] = np.random.permutation(np.resize(levels, 8))
        for g in range(8):
            far = levels[np.abs(levels - a[p, g]) >= 10]
            a[p, g + 8] = far[np.random.randint(len(far))]
    return np.exp2(a.ravel()).repeat(32)


def f64(x):
    return np.asarray(x).astype(np.float64)


def striped(idx):
    return np.tile(idx.reshape(-1, 16).T, (8, 1)).astype(np.uint16)


def unstriped(offs):
    return offs[:16].T.reshape(-1).astype(np.int64)


def striped8(idx):
    return np.concatenate([x.reshape(-1, 16).T for x in idx]).astype(np.uint16)


def runs(offs, k):
    lists = np.stack([offs[16 * r : 16 * r + 16].T.reshape(-1) for r in range(8)]).astype(np.int64)
    return lists[np.arange(k) % 512 // 64]


def pack_weight(w):
    k, n = w.shape
    w = f64(np.asarray(w, np.float32).astype(ml_dtypes.bfloat16)).reshape(k // 32, 32, n)
    amax = np.abs(w).max(1)
    byte = np.clip(np.where(amax > 0, np.frexp(amax)[1] - 1 + 127 - 7, 1), 1, 254)
    scaled = (w * np.exp2(127.0 - byte)[:, None, :]).reshape(k, n).astype(np.float32)
    words = np.ascontiguousarray(scaled.reshape(k // 512, 128, 4, n).transpose(0, 1, 3, 2)).astype(ml_dtypes.float8_e4m3fn).view(np.uint8)
    return words, np.ascontiguousarray(byte.astype(np.uint8).reshape(k // 512, 16, n))


def unpack_weight(words, scales):
    g, p, n, _ = words.shape
    vals = np.ascontiguousarray(words).view(ml_dtypes.float8_e4m3fn).astype(np.float64) * np.repeat(np.exp2(scales.astype(np.float64) - 127.0), 8, axis=1)[..., None]
    return vals.transpose(0, 1, 3, 2).reshape(g * 512, n)


K, T, S, N, H, U = 512, 2048, 512, 512, 512, 1024


def setup_inputs():
    n = np.random.standard_normal
    s = mx_kscale(K)[:, None]
    u = mx_kscale(H)
    packed_xT = pack_weight(n((K, T)) * s)
    return {
        "x_words": packed_xT[0],
        "x_scales": packed_xT[1],
        "w1": (n((K, H)) / np.sqrt(K) / s).astype(np.float32),
        "gn": (np.random.uniform(0.5, 1.5, (H, 1)) * u[:, None]).astype(np.float32),
        "w2": (n((H, N)) / np.sqrt(H) / u[:, None]).astype(np.float32),
        "mem": n((N, U)).astype(np.float32),
        "offs": striped(np.random.permutation(T)[:S]),
        "n1": striped8(np.stack([np.random.permutation(S) for _ in range(8)])),
        "n2": striped8(np.stack([np.random.permutation(S) for _ in range(8)])),
        "n3": striped8(np.stack([np.random.permutation(U)[:S] for _ in range(8)])),
    }


def reference(x_words, x_scales, w1, gn, w2, mem, offs, n1, n2, n3):
    xq = unpack_weight(x_words, x_scales)[:, unstriped(offs)]
    y = mxq(f64(w1), 0, "e4m3").T @ xq
    z = f64(gn) * ((y - (y[np.arange(H)[:, None], runs(n1, H)])) / (np.abs(y[np.arange(H)[:, None], runs(n2, H)] - y) + 0.5))
    h = mxq(f64(w2), 0, "e4m3").T @ mxq(z, 0, "e4m3")
    out = f64(mem).copy()
    out[np.arange(N)[:, None], runs(n3, N)] = h
    return out

@@ -1,0 +1,229 @@
+from contextlib import ExitStack
+
+import concourse.mybir as mybir
+
+K, T, S, H, N, U = 512, 2048, 512, 512, 512, 1024
+FLOPS = 2 * K * H * S + 2 * H * N * S
+
+F32 = mybir.dt.float32
+BF16 = mybir.dt.bfloat16
+I32 = mybir.dt.int32
+U32 = mybir.dt.uint32
+U16 = mybir.dt.uint16
+U8 = mybir.dt.uint8
+FP8X4 = mybir.dt.float8_e4m3fn_x4
+ALU = mybir.AluOpType
+ACT = mybir.ActivationFunctionType
+
+P = 128
+PACK = 4
+HALF = S // 2
+LIST_HALF = HALF // 16
+SCALAR_SHARE = 96
+
+
+def tile_picked_layfracpage_none_p_kernel(
+    tc, x_words, x_scales, w1, gn, w2, mem, offs, n1, n2, n3, out
+):
+    nc = tc.nc
+    with ExitStack() as ctx:
+        lists = ctx.enter_context(tc.tile_pool(name="lists", bufs=1))
+        keep = ctx.enter_context(tc.tile_pool(name="keep", bufs=1))
+        psum = ctx.enter_context(tc.psum_pool(name="psum", bufs=8))
+
+        def cols(half):
+            return slice(half * HALF, (half + 1) * HALF)
+
+        def entries(lst, half):
+            return lst[:, half * LIST_HALF : (half + 1) * LIST_HALF]
+
+        offs_sb = lists.tile([P, S // 16], U16, name="offs_sb")
+        n1_sb = lists.tile([P, S // 16], U16, name="n1_sb")
+        n2_sb = lists.tile([P, S // 16], U16, name="n2_sb")
+        n3_sb = lists.tile([P, S // 16], U16, name="n3_sb")
+        table_words = keep.tile([P, T], I32, name="table_words", align_bytes=64)
+        table_scales = keep.tile([P, T], U8, name="table_scales", align_bytes=64)
+        w1_raw = keep.tile([P, PACK, H], F32, name="w1_raw")
+        w2_raw = keep.tile([P, PACK, N], F32, name="w2_raw")
+        gain = keep.tile([P, PACK], F32, name="gain")
+        pages = [keep.tile([P, U], F32, name="page%d" % t) for t in range(PACK)]
+
+        nc.vector.memset(table_scales[:].bitcast(I32), 0)
+        nc.sync.dma_start(w1_raw[:], w1.rearrange("(p j) c -> p j c", j=PACK))
+        nc.sync.dma_start(offs_sb[:], offs)
+        for q in range(4):
+            nc.sync.dma_start(
+                table_scales[32 * q : 32 * q + 4, :].bitcast(I32),
+                x_scales[0, 4 * q : 4 * q + 4, :].bitcast(I32),
+            )
+        nc.sync.dma_start(table_words[:], x_words[0].rearrange("p n t -> p (n t)").bitcast(I32))
+        nc.sync.dma_start(n2_sb[:], n2)
+        nc.sync.dma_start(n1_sb[:], n1)
+        nc.sync.dma_start(w2_raw[:], w2.rearrange("(p j) c -> p j c", j=PACK))
+        nc.sync.dma_start(gain[:], gn.rearrange("(p t) o -> p (t o)", t=PACK))
+        nc.sync.dma_start(n3_sb[:], n3)
+        mem_rows = mem.rearrange("(p t) u -> t p u", t=PACK)
+        out_rows = out.rearrange("(p t) u -> t p u", t=PACK)
+        for t in range(PACK):
+            nc.sync.dma_start(pages[t][:], mem_rows[t])
+
+        x_scale = keep.tile([P, S], U8, name="x_scale", align_bytes=64)
+        nc.vector.tensor_copy(x_scale[:], table_scales[:].indirect(offs_sb[:]))
+
+        w1_dealt = keep.tile([P, PACK * H], BF16, name="w1_dealt", align_bytes=64)
+        w1_to = w1_dealt[:].rearrange("p (t m j) -> p m t j", t=PACK, j=PACK)
+        w1_from = w1_raw[:].rearrange("p j (m t) -> p m t j", t=PACK)
+        nc.scalar.copy(w1_to[:, :SCALAR_SHARE], w1_from[:, :SCALAR_SHARE])
+        nc.vector.tensor_copy(w1_to[:, SCALAR_SHARE:], w1_from[:, SCALAR_SHARE:])
+        w1_codes = keep.tile([P, H], U32, name="w1_codes", align_bytes=64)
+        w1_scale = keep.tile([P, H], U8, name="w1_scale", align_bytes=64)
+
+        def quantize_w1(a, b):
+            nc.vector.quantize_mx(
+                out=w1_codes[:, a * P : b * P].bitcast(FP8X4),
+                scales=w1_scale[:, a * P : b * P],
+                in_=w1_dealt[:, a * P * PACK : b * P * PACK],
+            )
+
+        quantize_w1(0, 1)
+        x_codes = keep.tile([P, S], U32, name="x_codes", align_bytes=64)
+        for half in range(2):
+            nc.vector.tensor_copy(
+                x_codes[:, cols(half)], table_words[:].bitcast(U32).indirect(entries(offs_sb, half))
+            )
+        quantize_w1(1, 2)
+        quantize_w1(2, 4)
+
+        def product(width, codes, scale, t, rhs_codes, rhs_scale):
+            acc = psum.tile([P, width], F32, name="acc", tag="acc")
+            rows = slice(t * P, (t + 1) * P)
+            nc.tensor.matmul_mx(
+                out=acc[:],
+                lhsT=codes[:, rows].bitcast(FP8X4),
+                lhsT_scale=scale[:, rows],
+                rhs=rhs_codes.bitcast(FP8X4),
+                rhs_scale=rhs_scale,
+                start=True,
+                stop=True,
+            )
+            return acc
+
+        y_window = [keep.tile([P, S], F32, name="y_window%d" % t) for t in range(PACK)]
+        y_plain = [keep.tile([P, S], F32, name="y_plain%d" % t) for t in range(PACK)]
+        y_late = []
+        for t in range(PACK):
+            if t == 0:
+                accs = [product(HALF, w1_codes, w1_scale, t, x_codes[:, cols(h)], x_scale[:, cols(h)]) for h in range(2)]
+                nc.scalar.copy(y_window[t][:, cols(0)], accs[0][:])
+                nc.scalar.copy(y_plain[t][:, cols(0)], accs[0][:])
+                nc.scalar.copy(y_window[t][:, cols(1)], accs[1][:])
+                y_late.append(accs[1][:])
+            else:
+                acc = product(S, w1_codes, w1_scale, t, x_codes[:], x_scale[:])
+                nc.scalar.copy(y_window[t][:], acc[:])
+                nc.scalar.copy(y_plain[t][:, cols(0)], acc[:, cols(0)])
+                y_late.append(acc[:, cols(1)])
+
+        neg_gain = keep.tile([P, PACK], F32, name="neg_gain")
+        nc.gpsimd.tensor_scalar(neg_gain[:], gain[:], -1.0, 0.0, ALU.mult, ALU.add)
+
+        def differences(t, half, num, den):
+            plain = y_plain[t][:, cols(half)]
+            nc.vector.tensor_tensor(den, y_window[t][:].indirect(entries(n2_sb, half)), plain, ALU.subtract)
+            nc.vector.tensor_tensor(num, y_window[t][:].indirect(entries(n1_sb, half)), plain, ALU.subtract)
+
+        def reciprocal(recip):
+            nc.scalar.activation(recip, recip, ACT.Abs_reciprocal_sqrt, bias=0.5)
+            nc.scalar.activation(recip, recip, ACT.Square)
+
+        def quotient(z_rows, nums, recip):
+            for t in range(PACK):
+                nc.vector.scalar_tensor_tensor(
+                    z_rows[:, t, :], nums[t], neg_gain[:, t : t + 1], recip[:, t, :], ALU.mult, ALU.mult
+                )
+
+        def interleave(z_rows, z_packed):
+            nc.scalar.copy(
+                z_packed[:].rearrange("p (c i t) -> p c t i", i=4, t=PACK),
+                z_rows[:].rearrange("p t (c i) -> p c t i", i=4),
+            )
+
+        def quantize_z(z_packed, half):
+            codes = keep.tile([P, HALF], U32, name="z_codes%d" % half, align_bytes=64)
+            scale = keep.tile([P, HALF], U8, name="z_scale%d" % half, align_bytes=64)
+            nc.vector.quantize_mx(out=codes[:].bitcast(FP8X4), scales=scale[:], in_=z_packed[:])
+            return codes, scale
+
+        w2_parts = []
+
+        def quantize_w2(pair):
+            dealt = keep.tile([P, 2 * P * PACK], BF16, name="w2_dealt%d" % pair, align_bytes=64)
+            for m in range(0, P, 32):
+                nc.scalar.copy(
+                    dealt[:].rearrange("p (t m j) -> p m t j", t=2, j=PACK)[:, m : m + 32],
+                    w2_raw[:].rearrange("p j (m t) -> p m t j", t=PACK)[:, m : m + 32, 2 * pair : 2 * pair + 2, :],
+                )
+            codes = keep.tile([P, 2 * P], U32, name="w2_codes%d" % pair, align_bytes=64)
+            scale = keep.tile([P, 2 * P], U8, name="w2_scale%d" % pair, align_bytes=64)
+            nc.vector.quantize_mx(out=codes[:].bitcast(FP8X4), scales=scale[:], in_=dealt[:])
+            w2_parts.append((codes, scale))
+
+        def put(t, half, z_codes, z_scale, tag):
+            codes, scale = w2_parts[t // 2]
+            acc = product(HALF, codes, scale, t % 2, z_codes[:], z_scale[:])
+            h_sb = keep.tile([P, HALF], F32, name="h_sb", tag=tag, align_bytes=64)
+            nc.scalar.copy(h_sb[:], acc[:])
+            nc.vector.tensor_copy(pages[t][:].indirect(entries(n3_sb, half)), h_sb[:])
+            if half == 1:
+                nc.sync.dma_start(out_rows[t], pages[t][:])
+
+        num0 = keep.tile([P, PACK, HALF], F32, name="num0", tag="reuse2", align_bytes=64)
+        den0 = [keep.tile([P, 2, HALF], F32, name="den0", tag="reuse%d" % i, align_bytes=64) for i in range(2)]
+        for t in range(PACK):
+            differences(t, 0, num0[:, t, :], den0[t // 2][:, t % 2, :])
+        recip0 = keep.tile([P, PACK, HALF], F32, name="recip0")
+        for t in range(2):
+            nc.scalar.copy(y_plain[t][:, cols(1)], y_late[t])
+        nc.scalar.activation(recip0[:, 0:2, :], den0[0][:], ACT.Abs)
+        reciprocal(recip0[:, 0:2, :])
+        for t in range(2, PACK):
+            nc.scalar.copy(y_plain[t][:, cols(1)], y_late[t])
+        nc.scalar.activation(recip0[:, 2:4, :], den0[1][:], ACT.Abs)
+        reciprocal(recip0[:, 2:4, :])
+
+        second = []
+
+        def second_differences(t):
+            both = keep.tile([P, 2, HALF], F32, name="both", tag="reuse%d" % t, align_bytes=64)
+            differences(t, 1, both[:, 0, :], both[:, 1, :])
+            second.append(both)
+
+        second_differences(0)
+        second_differences(1)
+        z_rows0 = keep.tile([P, PACK, HALF], BF16, name="z_rows0", align_bytes=64)
+        quotient(z_rows0, [num0[:, t, :] for t in range(PACK)], recip0)
+        quantize_w2(0)
+        second_differences(2)
+        z_packed0 = keep.tile([P, PACK * HALF], BF16, name="z_packed0", tag="reuse3", align_bytes=64)
+        interleave(z_rows0, z_packed0)
+        z_codes0, z_scale0 = quantize_z(z_packed0, 0)
+        second_differences(3)
+
+        recip1 = keep.tile([P, PACK, HALF], F32, name="recip1")
+        for t in range(2):
+            nc.scalar.activation(recip1[:, t, :], second[t][:, 1, :], ACT.Abs)
+        put(0, 0, z_codes0, z_scale0, "h00")
+        quantize_w2(1)
+        put(1, 0, z_codes0, z_scale0, "h10")
+        for t in range(2, PACK):
+            nc.scalar.activation(recip1[:, t, :], second[t][:, 1, :], ACT.Abs)
+        reciprocal(recip1[:])
+        z_rows1 = keep.tile([P, PACK, HALF], BF16, name="z_rows1", tag="reuse4", align_bytes=64)
+        quotient(z_rows1, [second[t][:, 0, :] for t in range(PACK)], recip1)
+        put(2, 0, z_codes0, z_scale0, "reuse0")
+        z_packed1 = keep.tile([P, PACK * HALF], BF16, name="z_packed1", align_bytes=64)
+        interleave(z_rows1, z_packed1)
+        z_codes1, z_scale1 = quantize_z(z_packed1, 1)
+        put(3, 0, z_codes0, z_scale0, "reuse4")
+        for t in range(PACK):
+            put(t, 1, z_codes1, z_scale1, "h%d1" % t)

@@ -1,6 +1,7 @@
 from contextlib import ExitStack
 
 import concourse.mybir as mybir
+from concourse.masks import make_identity
 
 K, T, S, H, N, U = 512, 2048, 512, 512, 512, 1024
 FLOPS = 2 * K * H * S + 2 * H * N * S
@@ -19,7 +20,6 @@ P = 128
 PACK = 4
 HALF = S // 2
 LIST_HALF = HALF // 16
-SCALAR_SHARE = 96
 
 
 def tile_picked_layfracpage_none_p_kernel(
@@ -41,16 +41,16 @@ def tile_picked_layfracpage_none_p_kernel(
         n1_sb = lists.tile([P, S // 16], U16, name="n1_sb")
         n2_sb = lists.tile([P, S // 16], U16, name="n2_sb")
         n3_sb = lists.tile([P, S // 16], U16, name="n3_sb")
-        table_words = keep.tile([P, T], I32, name="table_words", align_bytes=64)
-        table_scales = keep.tile([P, T], U8, name="table_scales", align_bytes=64)
+        table_words = keep.tile([P, T], I32, name="table_words", tag="table_words", align_bytes=64)
+        table_scales = keep.tile([P, T], U8, name="table_scales", tag="table_scales", align_bytes=64)
         w1_raw = keep.tile([P, PACK, H], F32, name="w1_raw")
         w2_raw = keep.tile([P, PACK, N], F32, name="w2_raw")
-        gain = keep.tile([P, PACK], F32, name="gain")
+        gain = keep.tile([P, PACK], F32, name="gain", tag="gain", align_bytes=64)
         pages = [keep.tile([P, U], F32, name="page%d" % t) for t in range(PACK)]
 
         nc.vector.memset(table_scales[:].bitcast(I32), 0)
-        nc.sync.dma_start(w1_raw[:], w1.rearrange("(p j) c -> p j c", j=PACK))
         nc.sync.dma_start(offs_sb[:], offs)
+        nc.sync.dma_start(w1_raw[:], w1.rearrange("(p j) c -> p j c", j=PACK))
         for q in range(4):
             nc.sync.dma_start(
                 table_scales[32 * q : 32 * q + 4, :].bitcast(I32),
@@ -58,47 +58,50 @@ def tile_picked_layfracpage_none_p_kernel(
             )
         nc.sync.dma_start(table_words[:], x_words[0].rearrange("p n t -> p (n t)").bitcast(I32))
         nc.sync.dma_start(n2_sb[:], n2)
+        nc.sync.dma_start(gain[:], gn.rearrange("(p t) o -> p (t o)", t=PACK))
         nc.sync.dma_start(n1_sb[:], n1)
         nc.sync.dma_start(w2_raw[:], w2.rearrange("(p j) c -> p j c", j=PACK))
-        nc.sync.dma_start(gain[:], gn.rearrange("(p t) o -> p (t o)", t=PACK))
         nc.sync.dma_start(n3_sb[:], n3)
         mem_rows = mem.rearrange("(p t) u -> t p u", t=PACK)
         out_rows = out.rearrange("(p t) u -> t p u", t=PACK)
         for t in range(PACK):
             nc.sync.dma_start(pages[t][:], mem_rows[t])
 
+        warm = keep.tile([P, 2], F32, name="warm")
+        nc.gpsimd.memset(warm[:, 0:1], 1.0)
+        nc.scalar.activation(warm[:, 1:2], warm[:, 0:1], ACT.Abs_reciprocal_sqrt)
+
+        identity = keep.tile([P, P], F32, name="identity")
+        make_identity(nc, identity[:])
+
         x_scale = keep.tile([P, S], U8, name="x_scale", align_bytes=64)
         nc.vector.tensor_copy(x_scale[:], table_scales[:].indirect(offs_sb[:]))
 
-        w1_dealt = keep.tile([P, PACK * H], BF16, name="w1_dealt", align_bytes=64)
-        w1_to = w1_dealt[:].rearrange("p (t m j) -> p m t j", t=PACK, j=PACK)
-        w1_from = w1_raw[:].rearrange("p j (m t) -> p m t j", t=PACK)
-        nc.scalar.copy(w1_to[:, :SCALAR_SHARE], w1_from[:, :SCALAR_SHARE])
-        nc.vector.tensor_copy(w1_to[:, SCALAR_SHARE:], w1_from[:, SCALAR_SHARE:])
-        w1_codes = keep.tile([P, H], U32, name="w1_codes", align_bytes=64)
-        w1_scale = keep.tile([P, H], U8, name="w1_scale", align_bytes=64)
-
-        def quantize_w1(a, b):
-            nc.vector.quantize_mx(
-                out=w1_codes[:, a * P : b * P].bitcast(FP8X4),
-                scales=w1_scale[:, a * P : b * P],
-                in_=w1_dealt[:, a * P * PACK : b * P * PACK],
+        def deal(raw, pair, codes_tag, tag):
+            dealt = keep.tile([P, 2 * P * PACK], BF16, name="dealt", tag=tag, align_bytes=64)
+            nc.scalar.copy(
+                dealt[:].rearrange("p (t m j) -> p m t j", t=2, j=PACK),
+                raw[:].rearrange("p j (m t) -> p m t j", t=PACK)[:, :, 2 * pair : 2 * pair + 2, :],
             )
+            codes = keep.tile([P, 2 * P], U32, name="codes", tag=codes_tag, align_bytes=64)
+            scale = keep.tile([P, 2 * P], U8, name="scale", tag=codes_tag + "_scale", align_bytes=64)
+            nc.vector.quantize_mx(out=codes[:].bitcast(FP8X4), scales=scale[:], in_=dealt[:])
+            return codes, scale
 
-        quantize_w1(0, 1)
-        x_codes = keep.tile([P, S], U32, name="x_codes", align_bytes=64)
+        w1_parts = [deal(w1_raw, 0, "table_scales", "w1_dealt0")]
+
+        x_codes = []
         for half in range(2):
-            nc.vector.tensor_copy(
-                x_codes[:, cols(half)], table_words[:].bitcast(U32).indirect(entries(offs_sb, half))
-            )
-        quantize_w1(1, 2)
-        quantize_w1(2, 4)
+            picked = keep.tile([P, HALF], U32, name="x_codes%d" % half, align_bytes=64)
+            nc.vector.tensor_copy(picked[:], table_words[:].bitcast(U32).indirect(entries(offs_sb, half)))
+            x_codes.append(picked)
+        w1_parts.append(deal(w1_raw, 1, "table_words", "w1_dealt1"))
 
-        def product(width, codes, scale, t, rhs_codes, rhs_scale):
-            acc = psum.tile([P, width], F32, name="acc", tag="acc")
-            rows = slice(t * P, (t + 1) * P)
+        def product(acc, parts, t, rhs_codes, rhs_scale):
+            codes, scale = parts[t // 2]
+            rows = slice(t % 2 * P, (t % 2 + 1) * P)
             nc.tensor.matmul_mx(
-                out=acc[:],
+                out=acc,
                 lhsT=codes[:, rows].bitcast(FP8X4),
                 lhsT_scale=scale[:, rows],
                 rhs=rhs_codes.bitcast(FP8X4),
@@ -106,47 +109,79 @@ def tile_picked_layfracpage_none_p_kernel(
                 start=True,
                 stop=True,
             )
-            return acc
 
-        y_window = [keep.tile([P, S], F32, name="y_window%d" % t) for t in range(PACK)]
         y_plain = [keep.tile([P, S], F32, name="y_plain%d" % t) for t in range(PACK)]
-        y_late = []
+        y_gained = [keep.tile([P, S], F32, name="y_gained%d" % t) for t in range(PACK)]
+        y_banks = []
         for t in range(PACK):
-            if t == 0:
-                accs = [product(HALF, w1_codes, w1_scale, t, x_codes[:, cols(h)], x_scale[:, cols(h)]) for h in range(2)]
-                nc.scalar.copy(y_window[t][:, cols(0)], accs[0][:])
-                nc.scalar.copy(y_plain[t][:, cols(0)], accs[0][:])
-                nc.scalar.copy(y_window[t][:, cols(1)], accs[1][:])
-                y_late.append(accs[1][:])
-            else:
-                acc = product(S, w1_codes, w1_scale, t, x_codes[:], x_scale[:])
-                nc.scalar.copy(y_window[t][:], acc[:])
-                nc.scalar.copy(y_plain[t][:, cols(0)], acc[:, cols(0)])
-                y_late.append(acc[:, cols(1)])
+            for part in [cols(0), cols(1)] if t == 0 else [slice(0, S)]:
+                acc = psum.tile([P, part.stop - part.start], F32, name="acc", tag="acc")
+                for first in range(part.start, part.stop, HALF):
+                    half = first // HALF
+                    here = slice(first - part.start, first - part.start + HALF)
+                    product(acc[:, here], w1_parts, t, x_codes[half][:], x_scale[:, cols(half)])
+                nc.scalar.copy(y_plain[t][:, part], acc[:])
+                y_banks.append((t, part, acc))
+        for t, part, acc in y_banks:
+            nc.scalar.activation(y_gained[t][:, part], acc[:], ACT.Copy, scale=gain[:, t : t + 1])
 
-        neg_gain = keep.tile([P, PACK], F32, name="neg_gain")
-        nc.gpsimd.tensor_scalar(neg_gain[:], gain[:], -1.0, 0.0, ALU.mult, ALU.add)
+        def banks():
+            return [psum.tile([P, PACK, P], F32, name="turned", tag="acc") for c in range(2)]
 
-        def differences(t, half, num, den):
-            plain = y_plain[t][:, cols(half)]
-            nc.vector.tensor_tensor(den, y_window[t][:].indirect(entries(n2_sb, half)), plain, ALU.subtract)
-            nc.vector.tensor_tensor(num, y_window[t][:].indirect(entries(n1_sb, half)), plain, ALU.subtract)
-
-        def reciprocal(recip):
-            nc.scalar.activation(recip, recip, ACT.Abs_reciprocal_sqrt, bias=0.5)
-            nc.scalar.activation(recip, recip, ACT.Square)
-
-        def quotient(z_rows, nums, recip):
-            for t in range(PACK):
-                nc.vector.scalar_tensor_tensor(
-                    z_rows[:, t, :], nums[t], neg_gain[:, t : t + 1], recip[:, t, :], ALU.mult, ALU.mult
+        def difference(window, lst, t, half, fetched, turned):
+            nc.vector.tensor_scalar(fetched, window[:].indirect(entries(lst, half)), -1.0, 0.0, ALU.mult, ALU.add)
+            for c in range(2):
+                first = half * HALF + c * P
+                nc.tensor.matmul(
+                    turned[c][:, t, :], window[:, first : first + P], identity[:], start=True, stop=False, is_transpose=True
+                )
+            for c in range(2):
+                nc.tensor.matmul(
+                    turned[c][:, t, :], fetched[:, c * P : (c + 1) * P], identity[:], start=False, stop=True, is_transpose=True
                 )
 
-        def interleave(z_rows, z_packed):
-            nc.scalar.copy(
-                z_packed[:].rearrange("p (c i t) -> p c t i", i=4, t=PACK),
-                z_rows[:].rearrange("p t (c i) -> p c t i", i=4),
-            )
+        def paired(bank):
+            return bank[:].rearrange("c (u e) p -> c u p e", e=2)
+
+        def flat(tile):
+            return tile[:].rearrange("c (u p e) -> c u p e", u=2, e=2)
+
+        def magnitude(den, tags):
+            size = [keep.tile([P, H], F32, name="size", tag=tag, align_bytes=64) for tag in tags]
+            for c in range(2):
+                nc.scalar.activation(flat(size[c]), paired(den[c]), ACT.Abs)
+            return size
+
+        def reciprocal(size, half):
+            recip = [
+                keep.tile([P, H], F32, name="recip", tag="recip%d%d" % (half, c), align_bytes=64) for c in range(2)
+            ]
+            for c in range(2):
+                nc.scalar.activation(recip[c][:], size[c][:], ACT.Abs_reciprocal_sqrt, bias=0.5)
+            for c in range(2):
+                nc.scalar.activation(recip[c][:], recip[c][:], ACT.Square)
+            return recip
+
+        def quotient(num, recip, half):
+            z_turned = [
+                keep.tile([P, H], BF16, name="z_turned", tag="z_turned%d%d" % (half, c), align_bytes=64) for c in range(2)
+            ]
+            for c in range(2):
+                nc.vector.tensor_tensor(flat(z_turned[c]), paired(num[c]), flat(recip[c]), ALU.mult)
+            return z_turned
+
+        def turn_back(z_turned, half):
+            z_packed = keep.tile([P, PACK * HALF], BF16, name="z_packed", tag="z_packed%d" % half, align_bytes=64)
+            for c in range(2):
+                words = z_turned[c][:].bitcast(F32)
+                back = psum.tile([P, 2, P], F32, name="back", tag="acc")
+                for u in range(2):
+                    nc.tensor.transpose(back[:, u, :], words[:, u * P : (u + 1) * P], identity[:])
+                nc.scalar.copy(
+                    z_packed[:].bitcast(F32)[:, c * 2 * P : (c + 1) * 2 * P].rearrange("p (c u) -> p c u", u=2),
+                    back[:].rearrange("p u c -> p c u"),
+                )
+            return z_packed
 
         def quantize_z(z_packed, half):
             codes = keep.tile([P, HALF], U32, name="z_codes%d" % half, align_bytes=64)
@@ -156,74 +191,50 @@ def tile_picked_layfracpage_none_p_kernel(
 
         w2_parts = []
 
-        def quantize_w2(pair):
-            dealt = keep.tile([P, 2 * P * PACK], BF16, name="w2_dealt%d" % pair, align_bytes=64)
-            for m in range(0, P, 32):
-                nc.scalar.copy(
-                    dealt[:].rearrange("p (t m j) -> p m t j", t=2, j=PACK)[:, m : m + 32],
-                    w2_raw[:].rearrange("p j (m t) -> p m t j", t=PACK)[:, m : m + 32, 2 * pair : 2 * pair + 2, :],
-                )
-            codes = keep.tile([P, 2 * P], U32, name="w2_codes%d" % pair, align_bytes=64)
-            scale = keep.tile([P, 2 * P], U8, name="w2_scale%d" % pair, align_bytes=64)
-            nc.vector.quantize_mx(out=codes[:].bitcast(FP8X4), scales=scale[:], in_=dealt[:])
-            w2_parts.append((codes, scale))
+        def quantize_w2(pair, tag):
+            w2_parts.append(deal(w2_raw, pair, "w2_codes%d" % pair, tag))
 
         def put(t, half, z_codes, z_scale, tag):
-            codes, scale = w2_parts[t // 2]
-            acc = product(HALF, codes, scale, t % 2, z_codes[:], z_scale[:])
+            acc = psum.tile([P, HALF], F32, name="acc", tag="acc")
+            product(acc[:], w2_parts, t, z_codes[:], z_scale[:])
             h_sb = keep.tile([P, HALF], F32, name="h_sb", tag=tag, align_bytes=64)
             nc.scalar.copy(h_sb[:], acc[:])
             nc.vector.tensor_copy(pages[t][:].indirect(entries(n3_sb, half)), h_sb[:])
             if half == 1:
                 nc.sync.dma_start(out_rows[t], pages[t][:])
 
-        num0 = keep.tile([P, PACK, HALF], F32, name="num0", tag="reuse2", align_bytes=64)
-        den0 = [keep.tile([P, 2, HALF], F32, name="den0", tag="reuse%d" % i, align_bytes=64) for i in range(2)]
+        def fetched_tile(tag, count=1):
+            return keep.tile([P, count, HALF], F32, name="fetched", tag=tag, align_bytes=64)
+
+        den0, num0 = banks(), banks()
         for t in range(PACK):
-            differences(t, 0, num0[:, t, :], den0[t // 2][:, t % 2, :])
-        recip0 = keep.tile([P, PACK, HALF], F32, name="recip0")
+            difference(y_plain[t], n2_sb, t, 0, fetched_tile("first%d" % t)[:, 0, :], den0)
+        for t in range(PACK):
+            difference(y_gained[t], n1_sb, t, 0, fetched_tile("second%d" % t)[:, 0, :], num0)
+        recip0 = reciprocal(magnitude(den0, ["size00", "size01"]), 0)
+        den1 = banks()
+        every = fetched_tile("gain", PACK)
+        for t in range(PACK):
+            difference(y_plain[t], n2_sb, t, 1, every[:, t, :], den1)
+        z_turned0 = quotient(num0, recip0, 0)
+        quantize_w2(0, "size01")
+        num1 = banks()
+        both = fetched_tile("recip01", 2)
         for t in range(2):
-            nc.scalar.copy(y_plain[t][:, cols(1)], y_late[t])
-        nc.scalar.activation(recip0[:, 0:2, :], den0[0][:], ACT.Abs)
-        reciprocal(recip0[:, 0:2, :])
+            difference(y_gained[t], n1_sb, t, 1, both[:, t, :], num1)
+        z_codes0, z_scale0 = quantize_z(turn_back(z_turned0, 0), 0)
+        both = fetched_tile("z_packed0", 2)
         for t in range(2, PACK):
-            nc.scalar.copy(y_plain[t][:, cols(1)], y_late[t])
-        nc.scalar.activation(recip0[:, 2:4, :], den0[1][:], ACT.Abs)
-        reciprocal(recip0[:, 2:4, :])
+            difference(y_gained[t], n1_sb, t, 1, both[:, t - 2, :], num1)
 
-        second = []
-
-        def second_differences(t):
-            both = keep.tile([P, 2, HALF], F32, name="both", tag="reuse%d" % t, align_bytes=64)
-            differences(t, 1, both[:, 0, :], both[:, 1, :])
-            second.append(both)
-
-        second_differences(0)
-        second_differences(1)
-        z_rows0 = keep.tile([P, PACK, HALF], BF16, name="z_rows0", align_bytes=64)
-        quotient(z_rows0, [num0[:, t, :] for t in range(PACK)], recip0)
-        quantize_w2(0)
-        second_differences(2)
-        z_packed0 = keep.tile([P, PACK * HALF], BF16, name="z_packed0", tag="reuse3", align_bytes=64)
-        interleave(z_rows0, z_packed0)
-        z_codes0, z_scale0 = quantize_z(z_packed0, 0)
-        second_differences(3)
-
-        recip1 = keep.tile([P, PACK, HALF], F32, name="recip1")
-        for t in range(2):
-            nc.scalar.activation(recip1[:, t, :], second[t][:, 1, :], ACT.Abs)
+        size1 = magnitude(den1, ["z_turned01", "z_turned00"])
         put(0, 0, z_codes0, z_scale0, "h00")
-        quantize_w2(1)
+        quantize_w2(1, "size01")
         put(1, 0, z_codes0, z_scale0, "h10")
-        for t in range(2, PACK):
-            nc.scalar.activation(recip1[:, t, :], second[t][:, 1, :], ACT.Abs)
-        reciprocal(recip1[:])
-        z_rows1 = keep.tile([P, PACK, HALF], BF16, name="z_rows1", tag="reuse4", align_bytes=64)
-        quotient(z_rows1, [second[t][:, 0, :] for t in range(PACK)], recip1)
-        put(2, 0, z_codes0, z_scale0, "reuse0")
-        z_packed1 = keep.tile([P, PACK * HALF], BF16, name="z_packed1", align_bytes=64)
-        interleave(z_rows1, z_packed1)
-        z_codes1, z_scale1 = quantize_z(z_packed1, 1)
-        put(3, 0, z_codes0, z_scale0, "reuse4")
+        recip1 = reciprocal(size1, 1)
+        z_turned1 = quotient(num1, recip1, 1)
+        put(2, 0, z_codes0, z_scale0, "recip10")
+        z_codes1, z_scale1 = quantize_z(turn_back(z_turned1, 1), 1)
+        put(3, 0, z_codes0, z_scale0, "z_turned11")
         for t in range(PACK):
             put(t, 1, z_codes1, z_scale1, "h%d1" % t)

@@ -189,10 +189,16 @@ def tile_picked_layfracpage_none_p_kernel(
             nc.vector.quantize_mx(out=codes[:].bitcast(FP8X4), scales=scale[:], in_=z_packed[:])
             return codes, scale
 
+        w2_dealt = keep.tile([P, PACK * N], BF16, name="w2_dealt", align_bytes=64)
+        nc.gpsimd.tensor_scalar(
+            w2_dealt[:].rearrange("p (t m j) -> p m t j", t=PACK, j=PACK),
+            w2_raw[:].rearrange("p j (m t) -> p m t j", t=PACK),
+            1.0,
+            0.0,
+            ALU.mult,
+            ALU.add,
+        )
         w2_parts = []
-
-        def quantize_w2(pair, tag):
-            w2_parts.append(deal(w2_raw, pair, "w2_codes%d" % pair, tag))
 
         def put(t, half, z_codes, z_scale, tag):
             acc = psum.tile([P, HALF], F32, name="acc", tag="acc")
@@ -217,7 +223,11 @@ def tile_picked_layfracpage_none_p_kernel(
         for t in range(PACK):
             difference(y_plain[t], n2_sb, t, 1, every[:, t, :], den1)
         z_turned0 = quotient(num0, recip0, 0)
-        quantize_w2(0, "size01")
+        w2_codes = keep.tile([P, N], U32, name="w2_codes", tag="recip00", align_bytes=64)
+        w2_scale = keep.tile([P, N], U8, name="w2_scale", align_bytes=64)
+        nc.vector.quantize_mx(out=w2_codes[:].bitcast(FP8X4), scales=w2_scale[:], in_=w2_dealt[:])
+        for pair in range(2):
+            w2_parts.append((w2_codes[:, cols(pair)], w2_scale[:, cols(pair)]))
         num1 = banks()
         both = fetched_tile("recip01", 2)
         for t in range(2):
@@ -229,7 +239,6 @@ def tile_picked_layfracpage_none_p_kernel(
 
         size1 = magnitude(den1, ["z_turned01", "z_turned00"])
         put(0, 0, z_codes0, z_scale0, "h00")
-        quantize_w2(1, "size01")
         put(1, 0, z_codes0, z_scale0, "h10")
         recip1 = reciprocal(size1, 1)
         z_turned1 = quotient(num1, recip1, 1)

@@ -200,6 +200,14 @@ def tile_picked_layfracpage_none_p_kernel(
         )
         w2_parts = []
 
+        def quantize_w2(pair, tag):
+            codes = keep.tile([P, 2 * P], U32, name="w2_codes", tag=tag, align_bytes=64)
+            scale = keep.tile([P, 2 * P], U8, name="w2_scale%d" % pair, align_bytes=64)
+            nc.vector.quantize_mx(
+                out=codes[:].bitcast(FP8X4), scales=scale[:], in_=w2_dealt[:, pair * 2 * N : (pair + 1) * 2 * N]
+            )
+            w2_parts.append((codes, scale))
+
         def put(t, half, z_codes, z_scale, tag):
             acc = psum.tile([P, HALF], F32, name="acc", tag="acc")
             product(acc[:], w2_parts, t, z_codes[:], z_scale[:])
@@ -223,11 +231,7 @@ def tile_picked_layfracpage_none_p_kernel(
         for t in range(PACK):
             difference(y_plain[t], n2_sb, t, 1, every[:, t, :], den1)
         z_turned0 = quotient(num0, recip0, 0)
-        w2_codes = keep.tile([P, N], U32, name="w2_codes", tag="recip00", align_bytes=64)
-        w2_scale = keep.tile([P, N], U8, name="w2_scale", align_bytes=64)
-        nc.vector.quantize_mx(out=w2_codes[:].bitcast(FP8X4), scales=w2_scale[:], in_=w2_dealt[:])
-        for pair in range(2):
-            w2_parts.append((w2_codes[:, cols(pair)], w2_scale[:, cols(pair)]))
+        quantize_w2(0, "recip00")
         num1 = banks()
         both = fetched_tile("recip01", 2)
         for t in range(2):
@@ -237,12 +241,21 @@ def tile_picked_layfracpage_none_p_kernel(
         for t in range(2, PACK):
             difference(y_gained[t], n1_sb, t, 1, both[:, t - 2, :], num1)
 
-        size1 = magnitude(den1, ["z_turned01", "z_turned00"])
+        size1 = magnitude(den1, ["size10", "z_turned01"])
         put(0, 0, z_codes0, z_scale0, "h00")
-        put(1, 0, z_codes0, z_scale0, "h10")
-        recip1 = reciprocal(size1, 1)
-        z_turned1 = quotient(num1, recip1, 1)
-        put(2, 0, z_codes0, z_scale0, "recip10")
+        quantize_w2(1, "z_packed0")
+        recip1 = [keep.tile([P, H], F32, name="recip1%d" % c) for c in range(2)]
+        for c in range(2):
+            nc.scalar.activation(recip1[c][:], size1[c][:], ACT.Abs_reciprocal_sqrt, bias=0.5)
+        z_turned1 = []
+        for c in range(2):
+            nc.scalar.activation(recip1[c][:], recip1[c][:], ACT.Square)
+            staged = keep.tile([P, H], F32, name="staged%d" % c)
+            nc.scalar.copy(flat(staged), paired(num1[c]))
+            turned = keep.tile([P, H], BF16, name="z_turned", tag="z_turned1%d" % c, align_bytes=64)
+            nc.gpsimd.tensor_tensor(turned[:], staged[:], recip1[c][:], ALU.mult)
+            z_turned1.append(turned)
+            put(1 + c, 0, z_codes0, z_scale0, "h%d0" % (1 + c))
         z_codes1, z_scale1 = quantize_z(turn_back(z_turned1, 1), 1)
         put(3, 0, z_codes0, z_scale0, "z_turned11")
         for t in range(PACK):

from contextlib import ExitStack

import concourse.mybir as mybir
from concourse.masks import make_identity

K, T, S, H, N, U = 512, 2048, 512, 512, 512, 1024
FLOPS = 2 * K * H * S + 2 * H * N * S

F32 = mybir.dt.float32
BF16 = mybir.dt.bfloat16
I32 = mybir.dt.int32
U32 = mybir.dt.uint32
U16 = mybir.dt.uint16
U8 = mybir.dt.uint8
FP8X4 = mybir.dt.float8_e4m3fn_x4
ALU = mybir.AluOpType
ACT = mybir.ActivationFunctionType

P = 128
PACK = 4
HALF = S // 2
LIST_HALF = HALF // 16


def tile_picked_layfracpage_none_p_kernel(
    tc, x_words, x_scales, w1, gn, w2, mem, offs, n1, n2, n3, out
):
    nc = tc.nc
    with ExitStack() as ctx:
        lists = ctx.enter_context(tc.tile_pool(name="lists", bufs=1))
        keep = ctx.enter_context(tc.tile_pool(name="keep", bufs=1))
        psum = ctx.enter_context(tc.psum_pool(name="psum", bufs=8))

        def cols(half):
            return slice(half * HALF, (half + 1) * HALF)

        def entries(lst, half):
            return lst[:, half * LIST_HALF : (half + 1) * LIST_HALF]

        offs_sb = lists.tile([P, S // 16], U16, name="offs_sb")
        n1_sb = lists.tile([P, S // 16], U16, name="n1_sb")
        n2_sb = lists.tile([P, S // 16], U16, name="n2_sb")
        n3_sb = lists.tile([P, S // 16], U16, name="n3_sb")
        table_words = keep.tile([P, T], I32, name="table_words", tag="table_words", align_bytes=64)
        table_scales = keep.tile([P, T], U8, name="table_scales", tag="table_scales", align_bytes=64)
        w1_raw = keep.tile([P, PACK, H], F32, name="w1_raw")
        w2_raw = keep.tile([P, PACK, N], F32, name="w2_raw")
        gain = keep.tile([P, PACK], F32, name="gain", tag="gain", align_bytes=64)
        pages = [keep.tile([P, U], F32, name="page%d" % t) for t in range(PACK)]

        nc.vector.memset(table_scales[:].bitcast(I32), 0)
        nc.sync.dma_start(offs_sb[:], offs)
        nc.sync.dma_start(w1_raw[:], w1.rearrange("(p j) c -> p j c", j=PACK))
        for q in range(4):
            nc.sync.dma_start(
                table_scales[32 * q : 32 * q + 4, :].bitcast(I32),
                x_scales[0, 4 * q : 4 * q + 4, :].bitcast(I32),
            )
        nc.sync.dma_start(table_words[:], x_words[0].rearrange("p n t -> p (n t)").bitcast(I32))
        nc.sync.dma_start(n2_sb[:], n2)
        nc.sync.dma_start(gain[:], gn.rearrange("(p t) o -> p (t o)", t=PACK))
        nc.sync.dma_start(n1_sb[:], n1)
        nc.sync.dma_start(w2_raw[:], w2.rearrange("(p j) c -> p j c", j=PACK))
        nc.sync.dma_start(n3_sb[:], n3)
        mem_rows = mem.rearrange("(p t) u -> t p u", t=PACK)
        out_rows = out.rearrange("(p t) u -> t p u", t=PACK)
        for t in range(PACK):
            nc.sync.dma_start(pages[t][:], mem_rows[t])

        warm = keep.tile([P, 2], F32, name="warm")
        nc.gpsimd.memset(warm[:, 0:1], 1.0)
        nc.scalar.activation(warm[:, 1:2], warm[:, 0:1], ACT.Abs_reciprocal_sqrt)

        identity = keep.tile([P, P], F32, name="identity")
        make_identity(nc, identity[:])

        x_scale = keep.tile([P, S], U8, name="x_scale", align_bytes=64)
        nc.vector.tensor_copy(x_scale[:], table_scales[:].indirect(offs_sb[:]))

        def deal(raw, pair, codes_tag, tag):
            dealt = keep.tile([P, 2 * P * PACK], BF16, name="dealt", tag=tag, align_bytes=64)
            nc.scalar.copy(
                dealt[:].rearrange("p (t m j) -> p m t j", t=2, j=PACK),
                raw[:].rearrange("p j (m t) -> p m t j", t=PACK)[:, :, 2 * pair : 2 * pair + 2, :],
            )
            codes = keep.tile([P, 2 * P], U32, name="codes", tag=codes_tag, align_bytes=64)
            scale = keep.tile([P, 2 * P], U8, name="scale", tag=codes_tag + "_scale", align_bytes=64)
            nc.vector.quantize_mx(out=codes[:].bitcast(FP8X4), scales=scale[:], in_=dealt[:])
            return codes, scale

        w1_parts = [deal(w1_raw, 0, "table_scales", "w1_dealt0")]

        x_codes = []
        for half in range(2):
            picked = keep.tile([P, HALF], U32, name="x_codes%d" % half, align_bytes=64)
            nc.vector.tensor_copy(picked[:], table_words[:].bitcast(U32).indirect(entries(offs_sb, half)))
            x_codes.append(picked)
        w1_parts.append(deal(w1_raw, 1, "table_words", "w1_dealt1"))

        def product(acc, parts, t, rhs_codes, rhs_scale):
            codes, scale = parts[t // 2]
            rows = slice(t % 2 * P, (t % 2 + 1) * P)
            nc.tensor.matmul_mx(
                out=acc,
                lhsT=codes[:, rows].bitcast(FP8X4),
                lhsT_scale=scale[:, rows],
                rhs=rhs_codes.bitcast(FP8X4),
                rhs_scale=rhs_scale,
                start=True,
                stop=True,
            )

        y_plain = [keep.tile([P, S], F32, name="y_plain%d" % t) for t in range(PACK)]
        y_gained = [keep.tile([P, S], F32, name="y_gained%d" % t) for t in range(PACK)]
        y_banks = []
        for t in range(PACK):
            for part in [cols(0), cols(1)] if t == 0 else [slice(0, S)]:
                acc = psum.tile([P, part.stop - part.start], F32, name="acc", tag="acc")
                for first in range(part.start, part.stop, HALF):
                    half = first // HALF
                    here = slice(first - part.start, first - part.start + HALF)
                    product(acc[:, here], w1_parts, t, x_codes[half][:], x_scale[:, cols(half)])
                nc.scalar.copy(y_plain[t][:, part], acc[:])
                y_banks.append((t, part, acc))
        for t, part, acc in y_banks:
            nc.scalar.activation(y_gained[t][:, part], acc[:], ACT.Copy, scale=gain[:, t : t + 1])

        def banks():
            return [psum.tile([P, PACK, P], F32, name="turned", tag="acc") for c in range(2)]

        def difference(window, lst, t, half, fetched, turned):
            nc.vector.tensor_scalar(fetched, window[:].indirect(entries(lst, half)), -1.0, 0.0, ALU.mult, ALU.add)
            for c in range(2):
                first = half * HALF + c * P
                nc.tensor.matmul(
                    turned[c][:, t, :], window[:, first : first + P], identity[:], start=True, stop=False, is_transpose=True
                )
            for c in range(2):
                nc.tensor.matmul(
                    turned[c][:, t, :], fetched[:, c * P : (c + 1) * P], identity[:], start=False, stop=True, is_transpose=True
                )

        def paired(bank):
            return bank[:].rearrange("c (u e) p -> c u p e", e=2)

        def flat(tile):
            return tile[:].rearrange("c (u p e) -> c u p e", u=2, e=2)

        def magnitude(den, tags):
            size = [keep.tile([P, H], F32, name="size", tag=tag, align_bytes=64) for tag in tags]
            for c in range(2):
                nc.scalar.activation(flat(size[c]), paired(den[c]), ACT.Abs)
            return size

        def reciprocal(size, half):
            recip = [
                keep.tile([P, H], F32, name="recip", tag="recip%d%d" % (half, c), align_bytes=64) for c in range(2)
            ]
            for c in range(2):
                nc.scalar.activation(recip[c][:], size[c][:], ACT.Abs_reciprocal_sqrt, bias=0.5)
            for c in range(2):
                nc.scalar.activation(recip[c][:], recip[c][:], ACT.Square)
            return recip

        def quotient(num, recip, half):
            z_turned = [
                keep.tile([P, H], BF16, name="z_turned", tag="z_turned%d%d" % (half, c), align_bytes=64) for c in range(2)
            ]
            for c in range(2):
                nc.vector.tensor_tensor(flat(z_turned[c]), paired(num[c]), flat(recip[c]), ALU.mult)
            return z_turned

        def turn_back(z_turned, half):
            z_packed = keep.tile([P, PACK * HALF], BF16, name="z_packed", tag="z_packed%d" % half, align_bytes=64)
            for c in range(2):
                words = z_turned[c][:].bitcast(F32)
                back = psum.tile([P, 2, P], F32, name="back", tag="acc")
                for u in range(2):
                    nc.tensor.transpose(back[:, u, :], words[:, u * P : (u + 1) * P], identity[:])
                nc.scalar.copy(
                    z_packed[:].bitcast(F32)[:, c * 2 * P : (c + 1) * 2 * P].rearrange("p (c u) -> p c u", u=2),
                    back[:].rearrange("p u c -> p c u"),
                )
            return z_packed

        def quantize_z(z_packed, half):
            codes = keep.tile([P, HALF], U32, name="z_codes%d" % half, align_bytes=64)
            scale = keep.tile([P, HALF], U8, name="z_scale%d" % half, align_bytes=64)
            nc.vector.quantize_mx(out=codes[:].bitcast(FP8X4), scales=scale[:], in_=z_packed[:])
            return codes, scale

        w2_dealt = keep.tile([P, PACK * N], BF16, name="w2_dealt", align_bytes=64)
        nc.gpsimd.tensor_scalar(
            w2_dealt[:].rearrange("p (t m j) -> p m t j", t=PACK, j=PACK),
            w2_raw[:].rearrange("p j (m t) -> p m t j", t=PACK),
            1.0,
            0.0,
            ALU.mult,
            ALU.add,
        )
        w2_parts = []

        def quantize_w2(pair, tag):
            codes = keep.tile([P, 2 * P], U32, name="w2_codes", tag=tag, align_bytes=64)
            scale = keep.tile([P, 2 * P], U8, name="w2_scale%d" % pair, align_bytes=64)
            nc.vector.quantize_mx(
                out=codes[:].bitcast(FP8X4), scales=scale[:], in_=w2_dealt[:, pair * 2 * N : (pair + 1) * 2 * N]
            )
            w2_parts.append((codes, scale))

        def put(t, half, z_codes, z_scale, tag):
            acc = psum.tile([P, HALF], F32, name="acc", tag="acc")
            product(acc[:], w2_parts, t, z_codes[:], z_scale[:])
            h_sb = keep.tile([P, HALF], F32, name="h_sb", tag=tag, align_bytes=64)
            nc.scalar.copy(h_sb[:], acc[:])
            nc.vector.tensor_copy(pages[t][:].indirect(entries(n3_sb, half)), h_sb[:])
            if half == 1:
                nc.sync.dma_start(out_rows[t], pages[t][:])

        def fetched_tile(tag, count=1):
            return keep.tile([P, count, HALF], F32, name="fetched", tag=tag, align_bytes=64)

        den0, num0 = banks(), banks()
        for t in range(PACK):
            difference(y_plain[t], n2_sb, t, 0, fetched_tile("first%d" % t)[:, 0, :], den0)
        for t in range(PACK):
            difference(y_gained[t], n1_sb, t, 0, fetched_tile("second%d" % t)[:, 0, :], num0)
        recip0 = reciprocal(magnitude(den0, ["size00", "size01"]), 0)
        den1 = banks()
        every = fetched_tile("gain", PACK)
        for t in range(PACK):
            difference(y_plain[t], n2_sb, t, 1, every[:, t, :], den1)
        z_turned0 = quotient(num0, recip0, 0)
        quantize_w2(0, "recip00")
        num1 = banks()
        both = fetched_tile("recip01", 2)
        for t in range(2):
            difference(y_gained[t], n1_sb, t, 1, both[:, t, :], num1)
        z_codes0, z_scale0 = quantize_z(turn_back(z_turned0, 0), 0)
        both = fetched_tile("z_packed0", 2)
        for t in range(2, PACK):
            difference(y_gained[t], n1_sb, t, 1, both[:, t - 2, :], num1)

        size1 = magnitude(den1, ["size10", "z_turned01"])
        put(0, 0, z_codes0, z_scale0, "h00")
        quantize_w2(1, "z_packed0")
        recip1 = [keep.tile([P, H], F32, name="recip1%d" % c) for c in range(2)]
        for c in range(2):
            nc.scalar.activation(recip1[c][:], size1[c][:], ACT.Abs_reciprocal_sqrt, bias=0.5)
        z_turned1 = []
        for c in range(2):
            nc.scalar.activation(recip1[c][:], recip1[c][:], ACT.Square)
            staged = keep.tile([P, H], F32, name="staged%d" % c)
            nc.scalar.copy(flat(staged), paired(num1[c]))
            turned = keep.tile([P, H], BF16, name="z_turned", tag="z_turned1%d" % c, align_bytes=64)
            nc.gpsimd.tensor_tensor(turned[:], staged[:], recip1[c][:], ALU.mult)
            z_turned1.append(turned)
            put(1 + c, 0, z_codes0, z_scale0, "h%d0" % (1 + c))
        z_codes1, z_scale1 = quantize_z(turn_back(z_turned1, 1), 1)
        put(3, 0, z_codes0, z_scale0, "z_turned11")
        for t in range(PACK):
            put(t, 1, z_codes1, z_scale1, "h%d1" % t)
